import numpy as np
import ml_dtypes


def mxq(x, axis, fmt="e4m3"):
    dtype, down = {"e4m3": (ml_dtypes.float8_e4m3fn, 7), "e5m2": (ml_dtypes.float8_e5m2, 14)}[fmt]
    v = np.moveaxis(np.asarray(x, np.float32).astype(ml_dtypes.bfloat16).astype(np.float64), axis, -1)
    blocks = v.reshape(v.shape[:-1] + (-1, 32))
    amax = np.abs(blocks).max(-1, keepdims=True)
    byte = np.maximum(np.where(amax > 0, np.frexp(amax)[1] - 1 + 127, 0) - down, 1)
    scale = np.exp2(byte - 127.0)
    codes = (blocks / scale).astype(np.float32).astype(dtype).astype(np.float64)
    return np.moveaxis((codes * scale).reshape(v.shape), -1, axis)


WIDE = False


def mx_kscale(k):
    if not WIDE:
        return np.ones(k)
    levels = np.array([10, -10, 5, -5, 0])
    if k % 512:
        return np.exp2(np.random.permutation(np.resize(levels, k // 32))).repeat(32)
    a = np.empty((k // 512, 16))
    for p in range(k // 512):
        a[p, :8] = np.random.permutation(np.resize(levels, 8))
        for g in range(8):
            far = levels[np.abs(levels - a[p, g]) >= 10]
            a[p, g + 8] = far[np.random.randint(len(far))]
    return np.exp2(a.ravel()).repeat(32)


def f64(x):
    return np.asarray(x).astype(np.float64)


def striped(idx):
    return np.tile(np.asarray(idx).reshape(-1, 16).T, (8, 1)).astype(np.uint16)


def unstriped(offs):
    return offs[:16].T.reshape(-1).astype(np.int64)


E2M1 = np.array([0.0, 0.5, 1.0, 1.5, 2.0, 3.0, 4.0, 6.0, -0.0, -0.5, -1.0, -1.5, -2.0, -3.0, -4.0, -6.0])


def pack_weight(w, fmt):
    k, n = w.shape
    w = f64(np.asarray(w, np.float32).astype(ml_dtypes.bfloat16)).reshape(k // 32, 32, n)
    amax = np.abs(w).max(1)
    if fmt == "e4m3":
        byte = np.frexp(amax)[1] - 1 + 127 - 7
    else:
        mant, ex = np.frexp(amax / 6.0)
        byte = np.where(mant > 0.5, ex, ex - 1) + 127
    byte = np.clip(np.where(amax > 0, byte, 1), 1, 254)
    scaled = (w * np.exp2(127.0 - byte)[:, None, :]).reshape(k, n).astype(np.float32)
    by_word = np.ascontiguousarray(scaled.reshape(k // 512, 128, 4, n).transpose(0, 1, 3, 2))
    if fmt == "e4m3":
        words = by_word.astype(ml_dtypes.float8_e4m3fn).view(np.uint8)
    else:
        c = by_word.astype(ml_dtypes.float4_e2m1fn).view(np.uint8) & 0xF
        words = (c[..., 0::2] | (c[..., 1::2] << 4)).reshape(k // 512, 128, 2 * n)
    return np.ascontiguousarray(words), np.ascontiguousarray(byte.astype(np.uint8).reshape(k // 512, 16, n))


def unpack_weight(words, scales, fmt):
    g, _, n = scales.shape
    words = np.ascontiguousarray(words).reshape(g, 128, n, -1)
    if fmt == "e4m3":
        vals = words.view(ml_dtypes.float8_e4m3fn).astype(np.float64)
    else:
        nib = np.empty((g, 128, n, 4), np.uint8)
        nib[..., 0::2] = words & 0xF
        nib[..., 1::2] = words >> 4
        vals = E2M1[nib]
    vals = vals * np.repeat(np.exp2(scales.astype(np.float64) - 127.0), 8, axis=1)[..., None]
    return vals.transpose(0, 1, 3, 2).reshape(g * 512, n)


def bf(x):
    return np.asarray(x, np.float32).astype(ml_dtypes.bfloat16)


def planes(Y):
    r, m = Y.shape
    b = f64(bf(Y)).reshape(r // 32, 32, m)
    amax = np.abs(b).max(1)
    byte = np.clip(np.where(amax > 0, np.frexp(amax)[1] - 1 + 127 - 7, 1), 1, 254)
    codes = (b * np.exp2(127.0 - byte)[:, None, :]).reshape(r, m).astype(np.float32).astype(ml_dtypes.float8_e4m3fn).view(np.uint8)
    words = codes.reshape(r // 512, 128, 4, m).transpose(0, 1, 3, 2)
    return np.ascontiguousarray(words), np.ascontiguousarray(byte.astype(np.uint8).reshape(r // 512, 16, m))


C, I, T, L, N = 2048, 512, 512, 512, 512


def setup_inputs():
    n = np.random.standard_normal
    idx = np.random.permutation(C)[:I]
    idx2 = np.random.permutation(C)[:I]
    fi = mx_kscale(I)
    fl = mx_kscale(L)
    wp = pack_weight(n((I, N)) * 1 / np.sqrt(I) * fi[:, None], "e4m3")
    cxp = pack_weight(n((L, T)) / fl[:, None], "e2m1")
    wcp = pack_weight(n((L, N)) * 1 / np.sqrt(L) * fl[:, None], "e4m3")
    return {
        "xt": (n((T, C))).astype(np.float32),
        "pf": (np.random.uniform(0.5, 2.0, (I, 1)) / fi[:, None]).astype(np.float32),
        "w_words": wp[0],
        "w_scales": wp[1],
        "cx_words": cxp[0],
        "cx_scales": cxp[1],
        "wc_words": wcp[0],
        "wc_scales": wcp[1],
        "offs": striped(idx),
        "offs2": striped(idx2),
    }


def reference(xt, pf, w_words, w_scales, cx_words, cx_scales, wc_words, wc_scales, offs, offs2):
    idx = unstriped(offs)
    idx2 = unstriped(offs2)
    wu = unpack_weight(w_words, w_scales, "e4m3")
    cxu = unpack_weight(cx_words, cx_scales, "e2m1")
    wcu = unpack_weight(wc_words, wc_scales, "e4m3")
    pr = f64(xt)[:, idx] * f64(xt)[:, idx2]
    pt = pr.T
    pw = pt * f64(pf)
    pwq = mxq(pw, 0, "e4m3")
    y = wu.T @ pwq + wcu.T @ cxu
    words, scales = planes(y)
    return y, words, scales

@@ -1,0 +1,236 @@
+from contextlib import ExitStack
+
+import concourse.mybir as mybir
+from concourse.masks import make_identity
+
+C, I, T, L, N = 2048, 512, 512, 512, 512
+FLOPS = 2 * (I + L) * N * T
+
+F32 = mybir.dt.float32
+BF16 = mybir.dt.bfloat16
+I32 = mybir.dt.int32
+U16 = mybir.dt.uint16
+U8 = mybir.dt.uint8
+E4M3X4 = mybir.dt.float8_e4m3fn_x4
+E2M1X4 = mybir.dt.float4_e2m1fn_x4
+MULT = mybir.AluOpType.mult
+
+P = 128
+PACK = 4
+TILES = T // P
+STORE_GROUPS = ((0, 1), (2,), (3,))
+HALF = I // 2
+BASE = 4096
+STEP = 1024
+SPARE = BASE + 4 * STEP
+
+
+def tile_list_feature_pairs_by_lists_pl_kernel(
+    tc, xt, pf, w_words, w_scales, cx_words, cx_scales, wc_words, wc_scales, offs, offs2, out_0, out_1, out_2
+):
+    nc = tc.nc
+    with ExitStack() as ctx:
+        keep = ctx.enter_context(tc.tile_pool(name="keep", bufs=1))
+        work = ctx.enter_context(tc.tile_pool(name="work", bufs=4))
+        shared = ctx.enter_context(tc.tile_pool(name="shared", bufs=1))
+        psum = ctx.enter_context(tc.psum_pool(name="psum", bufs=1))
+
+        list1 = keep.tile([P, I // 16], U16, name="list1")
+        list2 = keep.tile([P, I // 16], U16, name="list2")
+        pf_rows = keep.tile([P, PACK], F32, name="pf_rows")
+        x_tiles = [keep.tile([P, C], F32, name="x%d" % j) for j in range(TILES)]
+        w_raw = keep.tile([P, 2, N], I32, name="w_raw")
+        cx_codes = keep.tile([P, 2 * T], U8, name="cx_codes", align_bytes=64)
+        ws_raw = shared.tile([P, N], U8, name="ws_raw", offset=SPARE, align_bytes=64)
+        cx_plane = keep.tile([P, T], U8, name="cx_plane", align_bytes=64)
+
+        nc.gpsimd.memset(ws_raw[:].bitcast(I32), 0)
+        nc.gpsimd.memset(cx_plane[:].bitcast(I32), 0)
+
+        def load_plane(queue, plane, first_row, scales, quadrants):
+            for q in quadrants:
+                at = 32 * q + first_row
+                queue.dma_start(out=plane[at : at + 4, :].bitcast(I32), in_=scales[0, 4 * q : 4 * q + 4, :].bitcast(I32))
+
+        def load_x(j):
+            nc.sync.dma_start(out=x_tiles[j][:], in_=xt[j * P : (j + 1) * P, :])
+
+        nc.sync.dma_start(out=pf_rows[:], in_=pf.rearrange("(p j) o -> p (j o)", j=PACK))
+        nc.sync.dma_start(list1[:], offs)
+        nc.sync.dma_start(list2[:], offs2)
+        load_x(0)
+        load_plane(nc.sync, ws_raw, 0, wc_scales, range(4))
+        nc.sync.dma_start(out=w_raw[:, 0, :], in_=wc_words[0].rearrange("p n r -> p (n r)").bitcast(I32))
+        nc.sync.dma_start(out=w_raw[:, 1, :], in_=w_words[0].rearrange("p n r -> p (n r)").bitcast(I32))
+        load_x(1)
+        nc.sync.dma_start(out=cx_codes[:].bitcast(I32), in_=cx_words[0].bitcast(I32))
+        load_plane(nc.sync, cx_plane, 0, cx_scales, range(4))
+        load_x(2)
+        load_x(3)
+
+        ident = keep.tile([P, P], F32, name="ident")
+        make_identity(nc, ident[:])
+        load_plane(nc.gpsimd, ws_raw, 4, w_scales, range(4))
+
+        pf_bank = psum.tile([P, PACK, P], F32, name="pf_bank")
+        for j in range(PACK):
+            nc.tensor.transpose(pf_bank[:, j, :], pf_rows[:, j : j + 1].to_broadcast([P, P]), ident[:])
+        pf_all = keep.tile([P, I], F32, name="pf_all")
+        nc.vector.tensor_copy(out=pf_all[:].rearrange("t (p j) -> t p j", j=PACK), in_=pf_bank[:].rearrange("t j p -> t p j"))
+
+        dealt = {}
+        y_plane = keep.tile([P, T], U8, name="y_plane", align_bytes=64)
+        out_rows = out_0.rearrange("(p r) t -> p r t", r=PACK)
+        out_words = out_1[0].rearrange("p t r -> p (t r)").bitcast(I32)
+
+        def region(j):
+            return BASE + (j - 1) * STEP
+
+        def gather_first(j, h):
+            name = "first%d_%d" % (j, h)
+            if j + h == 0:
+                first = keep.tile([P, HALF], F32, name=name)
+            else:
+                at = region(1) - STEP // 2 if j == 0 else region(j + h)
+                first = shared.tile([P, HALF], F32, name=name, offset=at, align_bytes=64)
+            entries = list1[:, h * HALF // 16 : (h + 1) * HALF // 16]
+            nc.vector.tensor_tensor(first[:], x_tiles[j][:].indirect(entries), pf_all[:, h * HALF : (h + 1) * HALF], MULT)
+            return first
+
+        def gather_second(j, h, first, pw_pairs):
+            tag = "grouped%d" % (j - 1) if h == 1 and j > 0 else "pw%d_%d" % (j, h)
+            pw = keep.tile([P, HALF], F32, name="pw%d_%d" % (j, h), tag=tag, align_bytes=64)
+            entries = list2[:, h * HALF // 16 : (h + 1) * HALF // 16]
+            nc.vector.tensor_tensor(pw[:], x_tiles[j][:].indirect(entries), first[:], MULT)
+            nc.scalar.copy(
+                out=pw_pairs[:].rearrange("t (u p e) -> t p u e", u=2, e=2)[:, h * HALF // 4 : (h + 1) * HALF // 4],
+                in_=pw[:].rearrange("t (p u e) -> t p u e", u=2, e=2),
+            )
+
+        def turn(j, pw_pairs):
+            bank = psum.tile([P, 2, P], F32, name="turn_bank", bufs=3)
+            for u in range(2):
+                nc.tensor.transpose(bank[:, u, :], pw_pairs[:].bitcast(F32)[:, u * P : (u + 1) * P], ident[:])
+            grouped = keep.tile([P, P * PACK], BF16, name="grouped%d" % j, tag="grouped%d" % j, align_bytes=64)
+            nc.scalar.copy(out=grouped[:].bitcast(F32).rearrange("p (t u) -> p t u", u=2), in_=bank[:].rearrange("p u t -> p t u"))
+            return grouped
+
+        def deal_words():
+            w_dealt = shared.tile([P, 2, N], I32, name="w_dealt", offset=0, align_bytes=64)
+            dealt["w"] = w_dealt
+            nc.vector.tensor_copy(
+                out=w_dealt[:].rearrange("p w (r a b) -> p w a r b", r=PACK, b=4),
+                in_=w_raw[:].rearrange("p w (a b r) -> p w a r b", r=PACK, b=4),
+            )
+
+        def deal_scales():
+            ws_dealt = shared.tile([P, N], U8, name="ws_dealt", offset=region(1) + STEP // 2, align_bytes=64)
+            dealt["s"] = ws_dealt
+            nc.vector.tensor_copy(
+                out=ws_dealt[:].rearrange("p (r a b) -> p a r b", r=PACK, b=16),
+                in_=ws_raw[:].rearrange("p (a b r) -> p a r b", r=PACK, b=16),
+            )
+
+        def linear_part(j):
+            bank = psum.tile([P, PACK, P], F32, name="y_bank%d" % j)
+            for r in range(PACK):
+                cols = slice(r * P, (r + 1) * P)
+                nc.tensor.matmul_mx(
+                    out=bank[:, r, :],
+                    lhsT=dealt["w"][:, 0, cols].bitcast(E4M3X4),
+                    lhsT_scale=dealt["s"][:, cols],
+                    rhs=cx_codes[:, 2 * j * P : 2 * (j + 1) * P].bitcast(E2M1X4),
+                    rhs_scale=cx_plane[:, j * P : (j + 1) * P],
+                    start=(r == 0),
+                    stop=False,
+                )
+            return bank
+
+        def pair_part(j, grouped, bank):
+            if j < TILES - 1:
+                codes = shared.tile([P, P], I32, name="pw_codes%d" % j, offset=region(j + 1), align_bytes=64)
+            else:
+                codes = keep.tile([P, P], I32, name="pw_codes%d" % j, align_bytes=64)
+            if j == 0:
+                plane = shared.tile([P, P], U8, name="pw_plane0", offset=SPARE, align_bytes=64)
+            else:
+                plane = work.tile([P, P], U8, name="pw_plane", align_bytes=64)
+            nc.vector.quantize_mx(out=codes[:].bitcast(E4M3X4), scales=plane[:], in_=grouped[:])
+            for r in range(PACK):
+                cols = slice(r * P, (r + 1) * P)
+                nc.tensor.matmul_mx(
+                    out=bank[:, r, :],
+                    lhsT=dealt["w"][:, 1, cols].bitcast(E4M3X4),
+                    lhsT_scale=dealt["s"][4:P, cols],
+                    rhs=codes[:].bitcast(E4M3X4),
+                    rhs_scale=plane[:],
+                    start=False,
+                    stop=(r == PACK - 1),
+                )
+
+        y_tiles = {}
+        for group in STORE_GROUPS:
+            y_tiles[group] = keep.tile([P, PACK, P * len(group)], F32, name="y%d" % group[0])
+
+        def keep_y(j, bank):
+            group = [g for g in STORE_GROUPS if j in g][0]
+            at = (j - group[0]) * P
+            nc.scalar.copy(out=y_tiles[group][:, :, at : at + P], in_=bank[:])
+            if j == group[-1]:
+                nc.sync.dma_start(out=out_rows[:, :, group[0] * P : (j + 1) * P], in_=y_tiles[group][:])
+
+        y_grouped = {}
+        for group in STORE_GROUPS:
+            y_grouped[group] = keep.tile([P, P * len(group), PACK], BF16, name="y_grouped%d" % group[0], align_bytes=64)
+
+        def round_y(j, bank):
+            group = [g for g in STORE_GROUPS if j in g][0]
+            at = (j - group[0]) * P
+            cast = nc.vector.tensor_copy if j >= TILES - 2 else nc.scalar.copy
+            cast(out=y_grouped[group][:, at : at + P, :], in_=bank[:].rearrange("p r t -> p t r"))
+
+        def planes_of_y(group):
+            span = slice(group[0] * P, (group[-1] + 1) * P)
+            if group[0] == 0:
+                y_codes = shared.tile([P, P * len(group)], I32, name="y_codes0", offset=region(TILES), align_bytes=64)
+            else:
+                y_codes = keep.tile([P, P * len(group)], I32, name="y_codes%d" % group[0], align_bytes=64)
+            nc.vector.quantize_mx(
+                out=y_codes[:].bitcast(E4M3X4),
+                scales=y_plane[:, span],
+                in_=y_grouped[group][:].rearrange("p t r -> p (t r)"),
+            )
+            nc.sync.dma_start(out=out_words[:, span], in_=y_codes[:])
+
+        grouped = None
+        for j in range(TILES):
+            firsts = [gather_first(j, h) for h in range(2)]
+            pairs = work.tile([P, I], BF16, name="pw_pairs", align_bytes=64)
+            gather_second(j, 0, firsts[0], pairs)
+            if j == 1:
+                deal_scales()
+            if j > 0:
+                bank = linear_part(j - 1)
+                pair_part(j - 1, grouped, bank)
+            gather_second(j, 1, firsts[1], pairs)
+            grouped = turn(j, pairs)
+            if j == 0:
+                deal_words()
+            elif j < TILES - 1:
+                keep_y(j - 1, bank)
+                round_y(j - 1, bank)
+        last_bank = linear_part(TILES - 1)
+        pair_part(TILES - 1, grouped, last_bank)
+        round_y(TILES - 2, bank)
+        keep_y(TILES - 2, bank)
+        planes_of_y(STORE_GROUPS[0])
+        planes_of_y(STORE_GROUPS[1])
+        keep_y(TILES - 1, last_bank)
+        round_y(TILES - 1, last_bank)
+        planes_of_y(STORE_GROUPS[2])
+
+        for q in range(4):
+            queue = nc.sync if q % 2 == 0 else nc.scalar
+            queue.dma_start(
+                out=out_2[0, 4 * q : 4 * q + 4, :].bitcast(I32), in_=y_plane[32 * q : 32 * q + 4, :].bitcast(I32)
+            )

@@ -20,9 +20,10 @@ PACK = 4
 TILES = T // P
 STORE_GROUPS = ((0, 1), (2,), (3,))
 HALF = I // 2
-BASE = 4096
-STEP = 1024
-SPARE = BASE + 4 * STEP
+A_BASE = 4096
+A_STEP = 640
+B_BASE = 8192
+PF_BASE = 10240
 
 
 def tile_list_feature_pairs_by_lists_pl_kernel(
@@ -41,11 +42,11 @@ def tile_list_feature_pairs_by_lists_pl_kernel(
         x_tiles = [keep.tile([P, C], F32, name="x%d" % j) for j in range(TILES)]
         w_raw = keep.tile([P, 2, N], I32, name="w_raw")
         cx_codes = keep.tile([P, 2 * T], U8, name="cx_codes", align_bytes=64)
-        ws_raw = shared.tile([P, N], U8, name="ws_raw", offset=SPARE, align_bytes=64)
+        ws_raw = keep.tile([P, N], U8, name="ws_raw")
         cx_plane = keep.tile([P, T], U8, name="cx_plane", align_bytes=64)
 
         nc.gpsimd.memset(ws_raw[:].bitcast(I32), 0)
-        nc.gpsimd.memset(cx_plane[:].bitcast(I32), 0)
+        nc.vector.memset(cx_plane[:].bitcast(I32), 0)
 
         def load_plane(queue, plane, first_row, scales, quadrants):
             for q in quadrants:
@@ -59,24 +60,33 @@ def tile_list_feature_pairs_by_lists_pl_kernel(
         nc.sync.dma_start(list1[:], offs)
         nc.sync.dma_start(list2[:], offs2)
         load_x(0)
-        load_plane(nc.sync, ws_raw, 0, wc_scales, range(4))
         nc.sync.dma_start(out=w_raw[:, 0, :], in_=wc_words[0].rearrange("p n r -> p (n r)").bitcast(I32))
+        load_plane(nc.sync, ws_raw, 0, wc_scales, range(3))
         nc.sync.dma_start(out=w_raw[:, 1, :], in_=w_words[0].rearrange("p n r -> p (n r)").bitcast(I32))
+        load_plane(nc.sync, ws_raw, 0, wc_scales, (3,))
         load_x(1)
+        load_plane(nc.sync, ws_raw, 4, w_scales, (0,))
         nc.sync.dma_start(out=cx_codes[:].bitcast(I32), in_=cx_words[0].bitcast(I32))
-        load_plane(nc.sync, cx_plane, 0, cx_scales, range(4))
+        load_plane(nc.sync, ws_raw, 4, w_scales, (1, 2, 3))
+        load_plane(nc.sync, cx_plane, 0, cx_scales, (3,))
         load_x(2)
         load_x(3)
 
         ident = keep.tile([P, P], F32, name="ident")
         make_identity(nc, ident[:])
-        load_plane(nc.gpsimd, ws_raw, 4, w_scales, range(4))
+        load_plane(nc.gpsimd, cx_plane, 0, cx_scales, range(3))
 
         pf_bank = psum.tile([P, PACK, P], F32, name="pf_bank")
         for j in range(PACK):
             nc.tensor.transpose(pf_bank[:, j, :], pf_rows[:, j : j + 1].to_broadcast([P, P]), ident[:])
-        pf_all = keep.tile([P, I], F32, name="pf_all")
-        nc.vector.tensor_copy(out=pf_all[:].rearrange("t (p j) -> t p j", j=PACK), in_=pf_bank[:].rearrange("t j p -> t p j"))
+        pf_all = []
+        for h in range(2):
+            half = shared.tile([P, HALF], F32, name="pf_all%d" % h, offset=PF_BASE + 4 * HALF * h, align_bytes=64)
+            nc.vector.tensor_copy(
+                out=half[:].rearrange("t (p j) -> t p j", j=PACK),
+                in_=pf_bank[:].rearrange("t j p -> t p j")[:, h * P // 2 : (h + 1) * P // 2],
+            )
+            pf_all.append(half)
 
         dealt = {}
         y_plane = keep.tile([P, T], U8, name="y_plane", align_bytes=64)
@@ -84,21 +94,17 @@ def tile_list_feature_pairs_by_lists_pl_kernel(
         out_words = out_1[0].rearrange("p t r -> p (t r)").bitcast(I32)
 
         def region(j):
-            return BASE + (j - 1) * STEP
+            return A_BASE - 64 + j * A_STEP
 
         def gather_first(j, h):
-            name = "first%d_%d" % (j, h)
-            if j + h == 0:
-                first = keep.tile([P, HALF], F32, name=name)
-            else:
-                at = region(1) - STEP // 2 if j == 0 else region(j + h)
-                first = shared.tile([P, HALF], F32, name=name, offset=at, align_bytes=64)
+            at = region(j) if h == 0 else B_BASE
+            first = shared.tile([P, HALF], F32, name="first%d_%d" % (j, h), offset=at, align_bytes=64)
             entries = list1[:, h * HALF // 16 : (h + 1) * HALF // 16]
-            nc.vector.tensor_tensor(first[:], x_tiles[j][:].indirect(entries), pf_all[:, h * HALF : (h + 1) * HALF], MULT)
+            nc.vector.tensor_tensor(first[:], x_tiles[j][:].indirect(entries), pf_all[h][:], MULT)
             return first
 
         def gather_second(j, h, first, pw_pairs):
-            tag = "grouped%d" % (j - 1) if h == 1 and j > 0 else "pw%d_%d" % (j, h)
+            tag = "grouped%d" % (j - 1) if h == 1 and j == TILES - 1 else "pw%d_%d" % (j, h)
             pw = keep.tile([P, HALF], F32, name="pw%d_%d" % (j, h), tag=tag, align_bytes=64)
             entries = list2[:, h * HALF // 16 : (h + 1) * HALF // 16]
             nc.vector.tensor_tensor(pw[:], x_tiles[j][:].indirect(entries), first[:], MULT)
@@ -108,7 +114,7 @@ def tile_list_feature_pairs_by_lists_pl_kernel(
             )
 
         def turn(j, pw_pairs):
-            bank = psum.tile([P, 2, P], F32, name="turn_bank", bufs=3)
+            bank = psum.tile([P, 2, P], F32, name="turn_bank%d" % j, tag="turn%d" % (j % 3))
             for u in range(2):
                 nc.tensor.transpose(bank[:, u, :], pw_pairs[:].bitcast(F32)[:, u * P : (u + 1) * P], ident[:])
             grouped = keep.tile([P, P * PACK], BF16, name="grouped%d" % j, tag="grouped%d" % j, align_bytes=64)
@@ -124,7 +130,7 @@ def tile_list_feature_pairs_by_lists_pl_kernel(
             )
 
         def deal_scales():
-            ws_dealt = shared.tile([P, N], U8, name="ws_dealt", offset=region(1) + STEP // 2, align_bytes=64)
+            ws_dealt = shared.tile([P, N], U8, name="ws_dealt", offset=region(1) + P, align_bytes=64)
             dealt["s"] = ws_dealt
             nc.vector.tensor_copy(
                 out=ws_dealt[:].rearrange("p (r a b) -> p a r b", r=PACK, b=16),
@@ -132,40 +138,46 @@ def tile_list_feature_pairs_by_lists_pl_kernel(
             )
 
         def linear_part(j):
-            bank = psum.tile([P, PACK, P], F32, name="y_bank%d" % j)
+            if j < TILES - 1:
+                bank = psum.tile([P, PACK, P], F32, name="y_bank%d" % j, tag="y%d" % (j % 2))
+                banks = [bank]
+            else:
+                low = psum.tile([P, PACK // 2, P], F32, name="y_low", tag="y1")
+                high = psum.tile([P, PACK // 2, P], F32, name="y_high", tag="turn2")
+                banks = [low, high]
+            per = PACK // len(banks)
             for r in range(PACK):
                 cols = slice(r * P, (r + 1) * P)
                 nc.tensor.matmul_mx(
-                    out=bank[:, r, :],
+                    out=banks[r // per][:, r % per, :],
                     lhsT=dealt["w"][:, 0, cols].bitcast(E4M3X4),
                     lhsT_scale=dealt["s"][:, cols],
                     rhs=cx_codes[:, 2 * j * P : 2 * (j + 1) * P].bitcast(E2M1X4),
                     rhs_scale=cx_plane[:, j * P : (j + 1) * P],
-                    start=(r == 0),
+                    start=(r % per == 0),
                     stop=False,
                 )
-            return bank
+            return banks
 
-        def pair_part(j, grouped, bank):
+        def pair_part(j, grouped, banks):
+            per = PACK // len(banks)
+            codes = work.tile([P, P], I32, name="pw_codes", align_bytes=64)
             if j < TILES - 1:
-                codes = shared.tile([P, P], I32, name="pw_codes%d" % j, offset=region(j + 1), align_bytes=64)
+                at = region(j + 1) if j < TILES - 2 else PF_BASE + 4 * HALF
+                plane = shared.tile([P, P], U8, name="pw_plane%d" % j, offset=at, align_bytes=64)
             else:
-                codes = keep.tile([P, P], I32, name="pw_codes%d" % j, align_bytes=64)
-            if j == 0:
-                plane = shared.tile([P, P], U8, name="pw_plane0", offset=SPARE, align_bytes=64)
-            else:
-                plane = work.tile([P, P], U8, name="pw_plane", align_bytes=64)
+                plane = keep.tile([P, P], U8, name="pw_plane%d" % j, align_bytes=64)
             nc.vector.quantize_mx(out=codes[:].bitcast(E4M3X4), scales=plane[:], in_=grouped[:])
             for r in range(PACK):
                 cols = slice(r * P, (r + 1) * P)
                 nc.tensor.matmul_mx(
-                    out=bank[:, r, :],
+                    out=banks[r // per][:, r % per, :],
                     lhsT=dealt["w"][:, 1, cols].bitcast(E4M3X4),
                     lhsT_scale=dealt["s"][4:P, cols],
                     rhs=codes[:].bitcast(E4M3X4),
                     rhs_scale=plane[:],
                     start=False,
-                    stop=(r == PACK - 1),
+                    stop=(r % per == per - 1),
                 )
 
         y_tiles = {}
@@ -192,7 +204,7 @@ def tile_list_feature_pairs_by_lists_pl_kernel(
         def planes_of_y(group):
             span = slice(group[0] * P, (group[-1] + 1) * P)
             if group[0] == 0:
-                y_codes = shared.tile([P, P * len(group)], I32, name="y_codes0", offset=region(TILES), align_bytes=64)
+                y_codes = shared.tile([P, P * len(group)], I32, name="y_codes0", offset=B_BASE, align_bytes=64)
             else:
                 y_codes = keep.tile([P, P * len(group)], I32, name="y_codes%d" % group[0], align_bytes=64)
             nc.vector.quantize_mx(
@@ -207,26 +219,35 @@ def tile_list_feature_pairs_by_lists_pl_kernel(
             firsts = [gather_first(j, h) for h in range(2)]
             pairs = work.tile([P, I], BF16, name="pw_pairs", align_bytes=64)
             gather_second(j, 0, firsts[0], pairs)
-            if j == 1:
-                deal_scales()
-            if j > 0:
+            if j == TILES - 1:
                 bank = linear_part(j - 1)
                 pair_part(j - 1, grouped, bank)
             gather_second(j, 1, firsts[1], pairs)
+            previous = grouped
             grouped = turn(j, pairs)
             if j == 0:
                 deal_words()
             elif j < TILES - 1:
-                keep_y(j - 1, bank)
-                round_y(j - 1, bank)
+                if j == 1:
+                    deal_scales()
+                bank = linear_part(j - 1)
+                pair_part(j - 1, previous, bank)
+                keep_y(j - 1, bank[0])
+                round_y(j - 1, bank[0])
         last_bank = linear_part(TILES - 1)
         pair_part(TILES - 1, grouped, last_bank)
-        round_y(TILES - 2, bank)
-        keep_y(TILES - 2, bank)
+        round_y(TILES - 2, bank[0])
+        keep_y(TILES - 2, bank[0])
         planes_of_y(STORE_GROUPS[0])
         planes_of_y(STORE_GROUPS[1])
-        keep_y(TILES - 1, last_bank)
-        round_y(TILES - 1, last_bank)
+        last = STORE_GROUPS[2]
+        y_last = y_tiles[last]
+        nc.scalar.copy(out=y_last[:, 0:2, :], in_=last_bank[0][:])
+        nc.vector.tensor_copy(out=y_last[:, 2:4, :], in_=last_bank[1][:])
+        nc.sync.dma_start(out=out_rows[:, :, last[0] * P :], in_=y_last[:])
+        by_token = y_last[:].rearrange("p r t -> p t r")
+        nc.scalar.copy(out=y_grouped[last][:, : P // 2, :], in_=by_token[:, : P // 2, :])
+        nc.vector.tensor_copy(out=y_grouped[last][:, P // 2 :, :], in_=by_token[:, P // 2 :, :])
         planes_of_y(STORE_GROUPS[2])
 
         for q in range(4):

@@ -19,7 +19,7 @@ P = 128
 PACK = 4
 TILES = T // P
 STORE_GROUPS = ((0, 1), (2,), (3,))
-HALF = I // 2
+PIECES = (slice(0, 384), slice(384, I))
 A_BASE = 4096
 A_STEP = 640
 B_BASE = 8192
@@ -32,7 +32,6 @@ def tile_list_feature_pairs_by_lists_pl_kernel(
     nc = tc.nc
     with ExitStack() as ctx:
         keep = ctx.enter_context(tc.tile_pool(name="keep", bufs=1))
-        work = ctx.enter_context(tc.tile_pool(name="work", bufs=4))
         shared = ctx.enter_context(tc.tile_pool(name="shared", bufs=1))
         psum = ctx.enter_context(tc.psum_pool(name="psum", bufs=1))
 
@@ -58,35 +57,35 @@ def tile_list_feature_pairs_by_lists_pl_kernel(
 
         nc.sync.dma_start(out=pf_rows[:], in_=pf.rearrange("(p j) o -> p (j o)", j=PACK))
         nc.sync.dma_start(list1[:], offs)
-        nc.sync.dma_start(list2[:], offs2)
         load_x(0)
-        nc.sync.dma_start(out=w_raw[:, 0, :], in_=wc_words[0].rearrange("p n r -> p (n r)").bitcast(I32))
-        load_plane(nc.sync, ws_raw, 0, wc_scales, range(3))
-        nc.sync.dma_start(out=w_raw[:, 1, :], in_=w_words[0].rearrange("p n r -> p (n r)").bitcast(I32))
-        load_plane(nc.sync, ws_raw, 0, wc_scales, (3,))
+        nc.sync.dma_start(list2[:], offs2)
+        load_plane(nc.sync, ws_raw, 0, wc_scales, (0, 1))
         load_x(1)
+        nc.sync.dma_start(out=w_raw[:, 0, :], in_=wc_words[0].rearrange("p n r -> p (n r)").bitcast(I32))
+        nc.sync.dma_start(out=w_raw[:, 1, :], in_=w_words[0].rearrange("p n r -> p (n r)").bitcast(I32))
+        load_plane(nc.sync, ws_raw, 0, wc_scales, (2, 3))
         load_plane(nc.sync, ws_raw, 4, w_scales, (0,))
-        nc.sync.dma_start(out=cx_codes[:].bitcast(I32), in_=cx_words[0].bitcast(I32))
-        load_plane(nc.sync, ws_raw, 4, w_scales, (1, 2, 3))
-        load_plane(nc.sync, cx_plane, 0, cx_scales, (3,))
         load_x(2)
+        nc.sync.dma_start(out=cx_codes[:].bitcast(I32), in_=cx_words[0].bitcast(I32))
+        load_plane(nc.sync, cx_plane, 0, cx_scales, range(4))
         load_x(3)
 
         ident = keep.tile([P, P], F32, name="ident")
         make_identity(nc, ident[:])
-        load_plane(nc.gpsimd, cx_plane, 0, cx_scales, range(3))
+        load_plane(nc.gpsimd, ws_raw, 4, w_scales, (1, 2, 3))
 
         pf_bank = psum.tile([P, PACK, P], F32, name="pf_bank")
         for j in range(PACK):
             nc.tensor.transpose(pf_bank[:, j, :], pf_rows[:, j : j + 1].to_broadcast([P, P]), ident[:])
         pf_all = []
-        for h in range(2):
-            half = shared.tile([P, HALF], F32, name="pf_all%d" % h, offset=PF_BASE + 4 * HALF * h, align_bytes=64)
+        for h, piece in enumerate(PIECES):
+            width = piece.stop - piece.start
+            part = shared.tile([P, width], F32, name="pf_all%d" % h, offset=PF_BASE + 4 * piece.start, align_bytes=64)
             nc.vector.tensor_copy(
-                out=half[:].rearrange("t (p j) -> t p j", j=PACK),
-                in_=pf_bank[:].rearrange("t j p -> t p j")[:, h * P // 2 : (h + 1) * P // 2],
+                out=part[:].rearrange("t (p j) -> t p j", j=PACK),
+                in_=pf_bank[:].rearrange("t j p -> t p j")[:, piece.start // PACK : piece.stop // PACK],
             )
-            pf_all.append(half)
+            pf_all.append(part)
 
         dealt = {}
         y_plane = keep.tile([P, T], U8, name="y_plane", align_bytes=64)
@@ -94,23 +93,25 @@ def tile_list_feature_pairs_by_lists_pl_kernel(
         out_words = out_1[0].rearrange("p t r -> p (t r)").bitcast(I32)
 
         def region(j):
-            return A_BASE - 64 + j * A_STEP
+            return (4736, 4032, 4736, 4864)[j]
 
         def gather_first(j, h):
             at = region(j) if h == 0 else B_BASE
-            first = shared.tile([P, HALF], F32, name="first%d_%d" % (j, h), offset=at, align_bytes=64)
-            entries = list1[:, h * HALF // 16 : (h + 1) * HALF // 16]
+            piece = PIECES[h]
+            first = shared.tile([P, piece.stop - piece.start], F32, name="first%d_%d" % (j, h), offset=at, align_bytes=64)
+            entries = list1[:, piece.start // 16 : piece.stop // 16]
             nc.vector.tensor_tensor(first[:], x_tiles[j][:].indirect(entries), pf_all[h][:], MULT)
             return first
 
         def gather_second(j, h, first, pw_pairs):
             tag = "grouped%d" % (j - 1) if h == 1 and j == TILES - 1 else "pw%d_%d" % (j, h)
-            pw = keep.tile([P, HALF], F32, name="pw%d_%d" % (j, h), tag=tag, align_bytes=64)
-            entries = list2[:, h * HALF // 16 : (h + 1) * HALF // 16]
+            piece = PIECES[h]
+            pw = keep.tile([P, piece.stop - piece.start], F32, name="pw%d_%d" % (j, h), tag=tag, align_bytes=64)
+            entries = list2[:, piece.start // 16 : piece.stop // 16]
             nc.vector.tensor_tensor(pw[:], x_tiles[j][:].indirect(entries), first[:], MULT)
             nc.scalar.copy(
-                out=pw_pairs[:].rearrange("t (u p e) -> t p u e", u=2, e=2)[:, h * HALF // 4 : (h + 1) * HALF // 4],
-                in_=pw[:].rearrange("t (p u e) -> t p u e", u=2, e=2),
+                out=pw_pairs[:].rearrange("t (u a b e) -> t a u b e", u=2, b=4, e=2)[:, piece.start // 16 : piece.stop // 16],
+                in_=pw[:].rearrange("t (a b u e) -> t a u b e", u=2, b=4, e=2),
             )
 
         def turn(j, pw_pairs):
@@ -130,7 +131,7 @@ def tile_list_feature_pairs_by_lists_pl_kernel(
             )
 
         def deal_scales():
-            ws_dealt = shared.tile([P, N], U8, name="ws_dealt", offset=region(1) + P, align_bytes=64)
+            ws_dealt = shared.tile([P, N], U8, name="ws_dealt", offset=4224, align_bytes=64)
             dealt["s"] = ws_dealt
             nc.vector.tensor_copy(
                 out=ws_dealt[:].rearrange("p (r a b) -> p a r b", r=PACK, b=16),
@@ -139,11 +140,11 @@ def tile_list_feature_pairs_by_lists_pl_kernel(
 
         def linear_part(j):
             if j < TILES - 1:
-                bank = psum.tile([P, PACK, P], F32, name="y_bank%d" % j, tag="y%d" % (j % 2))
+                bank = psum.tile([P, PACK, P], F32, name="y_bank%d" % j, tag="y%d" % j if j < 2 else "turn2")
                 banks = [bank]
             else:
                 low = psum.tile([P, PACK // 2, P], F32, name="y_low", tag="y1")
-                high = psum.tile([P, PACK // 2, P], F32, name="y_high", tag="turn2")
+                high = psum.tile([P, PACK // 2, P], F32, name="y_high")
                 banks = [low, high]
             per = PACK // len(banks)
             for r in range(PACK):
@@ -161,9 +162,9 @@ def tile_list_feature_pairs_by_lists_pl_kernel(
 
         def pair_part(j, grouped, banks):
             per = PACK // len(banks)
-            codes = work.tile([P, P], I32, name="pw_codes", align_bytes=64)
+            codes = keep.tile([P, P], I32, name="pw_codes%d" % j, tag="codes%d" % j, align_bytes=64)
             if j < TILES - 1:
-                at = region(j + 1) if j < TILES - 2 else PF_BASE + 4 * HALF
+                at = (4096, 4736)[j] if j < TILES - 2 else PF_BASE + 4 * PIECES[1].start
                 plane = shared.tile([P, P], U8, name="pw_plane%d" % j, offset=at, align_bytes=64)
             else:
                 plane = keep.tile([P, P], U8, name="pw_plane%d" % j, align_bytes=64)
@@ -191,33 +192,30 @@ def tile_list_feature_pairs_by_lists_pl_kernel(
             if j == group[-1]:
                 nc.sync.dma_start(out=out_rows[:, :, group[0] * P : (j + 1) * P], in_=y_tiles[group][:])
 
-        y_grouped = {}
-        for group in STORE_GROUPS:
-            y_grouped[group] = keep.tile([P, P * len(group), PACK], BF16, name="y_grouped%d" % group[0], align_bytes=64)
-
         def round_y(j, bank):
-            group = [g for g in STORE_GROUPS if j in g][0]
-            at = (j - group[0]) * P
-            cast = nc.vector.tensor_copy if j >= TILES - 2 else nc.scalar.copy
-            cast(out=y_grouped[group][:, at : at + P, :], in_=bank[:].rearrange("p r t -> p t r"))
+            cast = nc.vector.tensor_copy if j > 0 else nc.scalar.copy
+            y_grouped = keep.tile([P, P, PACK], BF16, name="y_grouped%d" % j, align_bytes=64)
+            cast(out=y_grouped[:], in_=bank[:].rearrange("p r t -> p t r"))
+            return y_grouped
 
-        def planes_of_y(group):
-            span = slice(group[0] * P, (group[-1] + 1) * P)
-            if group[0] == 0:
-                y_codes = shared.tile([P, P * len(group)], I32, name="y_codes0", offset=B_BASE, align_bytes=64)
-            else:
-                y_codes = keep.tile([P, P * len(group)], I32, name="y_codes%d" % group[0], align_bytes=64)
-            nc.vector.quantize_mx(
-                out=y_codes[:].bitcast(E4M3X4),
-                scales=y_plane[:, span],
-                in_=y_grouped[group][:].rearrange("p t r -> p (t r)"),
+        def round_kept_y(y_grouped, y_kept):
+            nc.vector.tensor_copy(
+                out=y_grouped.rearrange("p (c i) r -> p c r i", i=4), in_=y_kept.rearrange("p r (c i) -> p c r i", i=4)
             )
-            nc.sync.dma_start(out=out_words[:, span], in_=y_codes[:])
+
+        def planes_of_y(y_codes, first_token, y_grouped):
+            tokens = y_grouped.shape[1]
+            nc.vector.quantize_mx(
+                out=y_codes.bitcast(E4M3X4),
+                scales=y_plane[:, first_token : first_token + tokens],
+                in_=y_grouped.rearrange("p t r -> p (t r)"),
+            )
 
         grouped = None
         for j in range(TILES):
             firsts = [gather_first(j, h) for h in range(2)]
-            pairs = work.tile([P, I], BF16, name="pw_pairs", align_bytes=64)
+            tag = "codes%d" % (j - 2) if j >= 2 else "pairs%d" % j
+            pairs = keep.tile([P, I], BF16, name="pw_pairs%d" % j, tag=tag, align_bytes=64)
             gather_second(j, 0, firsts[0], pairs)
             if j == TILES - 1:
                 bank = linear_part(j - 1)
@@ -225,30 +223,41 @@ def tile_list_feature_pairs_by_lists_pl_kernel(
             gather_second(j, 1, firsts[1], pairs)
             previous = grouped
             grouped = turn(j, pairs)
-            if j == 0:
-                deal_words()
-            elif j < TILES - 1:
+            if 0 < j < TILES - 1:
                 if j == 1:
+                    deal_words()
                     deal_scales()
                 bank = linear_part(j - 1)
                 pair_part(j - 1, previous, bank)
                 keep_y(j - 1, bank[0])
-                round_y(j - 1, bank[0])
+                if j == 1:
+                    y_grouped0 = round_y(0, bank[0])
         last_bank = linear_part(TILES - 1)
         pair_part(TILES - 1, grouped, last_bank)
-        round_y(TILES - 2, bank[0])
-        keep_y(TILES - 2, bank[0])
-        planes_of_y(STORE_GROUPS[0])
-        planes_of_y(STORE_GROUPS[1])
+        y_grouped1 = shared.tile([P, P, PACK], BF16, name="y_grouped1", offset=B_BASE + 256, align_bytes=64)
+        round_kept_y(y_grouped1[:], y_tiles[STORE_GROUPS[0]][:, :, P:])
+        y_codes01 = shared.tile([P, 2 * P], I32, name="y_codes01", offset=B_BASE + 256 - 8 * P, align_bytes=64)
+        planes_of_y(y_codes01[:, :P], 0, y_grouped0[:])
+        y_grouped2 = round_y(2, bank[0])
+        keep_y(2, bank[0])
+        planes_of_y(y_codes01[:, P:], P, y_grouped1[:])
+        nc.sync.dma_start(out=out_words[:, : 2 * P], in_=y_codes01[:])
+        y_codes2 = keep.tile([P, P], I32, name="y_codes2", align_bytes=64)
+        planes_of_y(y_codes2[:], 2 * P, y_grouped2[:])
+        nc.sync.dma_start(out=out_words[:, 2 * P : 3 * P], in_=y_codes2[:])
         last = STORE_GROUPS[2]
         y_last = y_tiles[last]
-        nc.scalar.copy(out=y_last[:, 0:2, :], in_=last_bank[0][:])
-        nc.vector.tensor_copy(out=y_last[:, 2:4, :], in_=last_bank[1][:])
+        nc.vector.tensor_copy(out=y_last[:, 0:2, :], in_=last_bank[0][:])
+        nc.scalar.copy(out=y_last[:, 2:4, :], in_=last_bank[1][:])
         nc.sync.dma_start(out=out_rows[:, :, last[0] * P :], in_=y_last[:])
-        by_token = y_last[:].rearrange("p r t -> p t r")
-        nc.scalar.copy(out=y_grouped[last][:, : P // 2, :], in_=by_token[:, : P // 2, :])
-        nc.vector.tensor_copy(out=y_grouped[last][:, P // 2 :, :], in_=by_token[:, P // 2 :, :])
-        planes_of_y(STORE_GROUPS[2])
+        y_grouped3 = keep.tile([P, P, PACK], BF16, name="y_grouped3", align_bytes=64)
+        y_codes3 = keep.tile([P, P], I32, name="y_codes3", align_bytes=64)
+        halves = [slice(h * P // 2, (h + 1) * P // 2) for h in range(2)]
+        for tokens in halves:
+            round_kept_y(y_grouped3[:, tokens, :], y_last[:, :, tokens])
+        for tokens in halves:
+            planes_of_y(y_codes3[:, tokens], last[0] * P + tokens.start, y_grouped3[:, tokens, :])
+        nc.sync.dma_start(out=out_words[:, last[0] * P :], in_=y_codes3[:])
 
         for q in range(4):
             queue = nc.sync if q % 2 == 0 else nc.scalar

from contextlib import ExitStack

import concourse.mybir as mybir
from concourse.masks import make_identity

C, I, T, L, N = 2048, 512, 512, 512, 512
FLOPS = 2 * (I + L) * N * T

F32 = mybir.dt.float32
BF16 = mybir.dt.bfloat16
I32 = mybir.dt.int32
U16 = mybir.dt.uint16
U8 = mybir.dt.uint8
E4M3X4 = mybir.dt.float8_e4m3fn_x4
E2M1X4 = mybir.dt.float4_e2m1fn_x4
MULT = mybir.AluOpType.mult

P = 128
PACK = 4
TILES = T // P
STORE_GROUPS = ((0, 1), (2,), (3,))
PIECES = (slice(0, 384), slice(384, I))
A_BASE = 4096
A_STEP = 640
B_BASE = 8192
PF_BASE = 10240


def tile_list_feature_pairs_by_lists_pl_kernel(
    tc, xt, pf, w_words, w_scales, cx_words, cx_scales, wc_words, wc_scales, offs, offs2, out_0, out_1, out_2
):
    nc = tc.nc
    with ExitStack() as ctx:
        keep = ctx.enter_context(tc.tile_pool(name="keep", bufs=1))
        shared = ctx.enter_context(tc.tile_pool(name="shared", bufs=1))
        psum = ctx.enter_context(tc.psum_pool(name="psum", bufs=1))

        list1 = keep.tile([P, I // 16], U16, name="list1")
        list2 = keep.tile([P, I // 16], U16, name="list2")
        pf_rows = keep.tile([P, PACK], F32, name="pf_rows")
        x_tiles = [keep.tile([P, C], F32, name="x%d" % j) for j in range(TILES)]
        w_raw = keep.tile([P, 2, N], I32, name="w_raw")
        cx_codes = keep.tile([P, 2 * T], U8, name="cx_codes", align_bytes=64)
        ws_raw = keep.tile([P, N], U8, name="ws_raw")
        cx_plane = keep.tile([P, T], U8, name="cx_plane", align_bytes=64)

        nc.gpsimd.memset(ws_raw[:].bitcast(I32), 0)
        nc.vector.memset(cx_plane[:].bitcast(I32), 0)

        def load_plane(queue, plane, first_row, scales, quadrants):
            for q in quadrants:
                at = 32 * q + first_row
                queue.dma_start(out=plane[at : at + 4, :].bitcast(I32), in_=scales[0, 4 * q : 4 * q + 4, :].bitcast(I32))

        def load_x(j):
            nc.sync.dma_start(out=x_tiles[j][:], in_=xt[j * P : (j + 1) * P, :])

        nc.sync.dma_start(out=pf_rows[:], in_=pf.rearrange("(p j) o -> p (j o)", j=PACK))
        nc.sync.dma_start(list1[:], offs)
        load_x(0)
        nc.sync.dma_start(list2[:], offs2)
        load_plane(nc.sync, ws_raw, 0, wc_scales, (0, 1))
        load_x(1)
        nc.sync.dma_start(out=w_raw[:, 0, :], in_=wc_words[0].rearrange("p n r -> p (n r)").bitcast(I32))
        nc.sync.dma_start(out=w_raw[:, 1, :], in_=w_words[0].rearrange("p n r -> p (n r)").bitcast(I32))
        load_plane(nc.sync, ws_raw, 0, wc_scales, (2, 3))
        load_plane(nc.sync, ws_raw, 4, w_scales, (0,))
        load_x(2)
        nc.sync.dma_start(out=cx_codes[:].bitcast(I32), in_=cx_words[0].bitcast(I32))
        load_plane(nc.sync, cx_plane, 0, cx_scales, range(4))
        load_x(3)

        ident = keep.tile([P, P], F32, name="ident")
        make_identity(nc, ident[:])
        load_plane(nc.gpsimd, ws_raw, 4, w_scales, (1, 2, 3))

        pf_bank = psum.tile([P, PACK, P], F32, name="pf_bank")
        for j in range(PACK):
            nc.tensor.transpose(pf_bank[:, j, :], pf_rows[:, j : j + 1].to_broadcast([P, P]), ident[:])
        pf_all = []
        for h, piece in enumerate(PIECES):
            width = piece.stop - piece.start
            part = shared.tile([P, width], F32, name="pf_all%d" % h, offset=PF_BASE + 4 * piece.start, align_bytes=64)
            nc.vector.tensor_copy(
                out=part[:].rearrange("t (p j) -> t p j", j=PACK),
                in_=pf_bank[:].rearrange("t j p -> t p j")[:, piece.start // PACK : piece.stop // PACK],
            )
            pf_all.append(part)

        dealt = {}
        y_plane = keep.tile([P, T], U8, name="y_plane", align_bytes=64)
        out_rows = out_0.rearrange("(p r) t -> p r t", r=PACK)
        out_words = out_1[0].rearrange("p t r -> p (t r)").bitcast(I32)

        def region(j):
            return (4736, 4032, 4736, 4864)[j]

        def gather_first(j, h):
            at = region(j) if h == 0 else B_BASE
            piece = PIECES[h]
            first = shared.tile([P, piece.stop - piece.start], F32, name="first%d_%d" % (j, h), offset=at, align_bytes=64)
            entries = list1[:, piece.start // 16 : piece.stop // 16]
            nc.vector.tensor_tensor(first[:], x_tiles[j][:].indirect(entries), pf_all[h][:], MULT)
            return first

        def gather_second(j, h, first, pw_pairs):
            tag = "grouped%d" % (j - 1) if h == 1 and j == TILES - 1 else "pw%d_%d" % (j, h)
            piece = PIECES[h]
            pw = keep.tile([P, piece.stop - piece.start], F32, name="pw%d_%d" % (j, h), tag=tag, align_bytes=64)
            entries = list2[:, piece.start // 16 : piece.stop // 16]
            nc.vector.tensor_tensor(pw[:], x_tiles[j][:].indirect(entries), first[:], MULT)
            nc.scalar.copy(
                out=pw_pairs[:].rearrange("t (u a b e) -> t a u b e", u=2, b=4, e=2)[:, piece.start // 16 : piece.stop // 16],
                in_=pw[:].rearrange("t (a b u e) -> t a u b e", u=2, b=4, e=2),
            )

        def turn(j, pw_pairs):
            bank = psum.tile([P, 2, P], F32, name="turn_bank%d" % j, tag="turn%d" % (j % 3))
            for u in range(2):
                nc.tensor.transpose(bank[:, u, :], pw_pairs[:].bitcast(F32)[:, u * P : (u + 1) * P], ident[:])
            grouped = keep.tile([P, P * PACK], BF16, name="grouped%d" % j, tag="grouped%d" % j, align_bytes=64)
            nc.scalar.copy(out=grouped[:].bitcast(F32).rearrange("p (t u) -> p t u", u=2), in_=bank[:].rearrange("p u t -> p t u"))
            return grouped

        def deal_words():
            w_dealt = shared.tile([P, 2, N], I32, name="w_dealt", offset=0, align_bytes=64)
            dealt["w"] = w_dealt
            nc.vector.tensor_copy(
                out=w_dealt[:].rearrange("p w (r a b) -> p w a r b", r=PACK, b=4),
                in_=w_raw[:].rearrange("p w (a b r) -> p w a r b", r=PACK, b=4),
            )

        def deal_scales():
            ws_dealt = shared.tile([P, N], U8, name="ws_dealt", offset=4224, align_bytes=64)
            dealt["s"] = ws_dealt
            nc.vector.tensor_copy(
                out=ws_dealt[:].rearrange("p (r a b) -> p a r b", r=PACK, b=16),
                in_=ws_raw[:].rearrange("p (a b r) -> p a r b", r=PACK, b=16),
            )

        def linear_part(j):
            if j < TILES - 1:
                bank = psum.tile([P, PACK, P], F32, name="y_bank%d" % j, tag="y%d" % j if j < 2 else "turn2")
                banks = [bank]
            else:
                low = psum.tile([P, PACK // 2, P], F32, name="y_low", tag="y1")
                high = psum.tile([P, PACK // 2, P], F32, name="y_high")
                banks = [low, high]
            per = PACK // len(banks)
            for r in range(PACK):
                cols = slice(r * P, (r + 1) * P)
                nc.tensor.matmul_mx(
                    out=banks[r // per][:, r % per, :],
                    lhsT=dealt["w"][:, 0, cols].bitcast(E4M3X4),
                    lhsT_scale=dealt["s"][:, cols],
                    rhs=cx_codes[:, 2 * j * P : 2 * (j + 1) * P].bitcast(E2M1X4),
                    rhs_scale=cx_plane[:, j * P : (j + 1) * P],
                    start=(r % per == 0),
                    stop=False,
                )
            return banks

        def pair_part(j, grouped, banks):
            per = PACK // len(banks)
            codes = keep.tile([P, P], I32, name="pw_codes%d" % j, tag="codes%d" % j, align_bytes=64)
            if j < TILES - 1:
                at = (4096, 4736)[j] if j < TILES - 2 else PF_BASE + 4 * PIECES[1].start
                plane = shared.tile([P, P], U8, name="pw_plane%d" % j, offset=at, align_bytes=64)
            else:
                plane = keep.tile([P, P], U8, name="pw_plane%d" % j, align_bytes=64)
            nc.vector.quantize_mx(out=codes[:].bitcast(E4M3X4), scales=plane[:], in_=grouped[:])
            for r in range(PACK):
                cols = slice(r * P, (r + 1) * P)
                nc.tensor.matmul_mx(
                    out=banks[r // per][:, r % per, :],
                    lhsT=dealt["w"][:, 1, cols].bitcast(E4M3X4),
                    lhsT_scale=dealt["s"][4:P, cols],
                    rhs=codes[:].bitcast(E4M3X4),
                    rhs_scale=plane[:],
                    start=False,
                    stop=(r % per == per - 1),
                )

        y_tiles = {}
        for group in STORE_GROUPS:
            y_tiles[group] = keep.tile([P, PACK, P * len(group)], F32, name="y%d" % group[0])

        def keep_y(j, bank):
            group = [g for g in STORE_GROUPS if j in g][0]
            at = (j - group[0]) * P
            nc.scalar.copy(out=y_tiles[group][:, :, at : at + P], in_=bank[:])
            if j == group[-1]:
                nc.sync.dma_start(out=out_rows[:, :, group[0] * P : (j + 1) * P], in_=y_tiles[group][:])

        def round_y(j, bank):
            cast = nc.vector.tensor_copy if j > 0 else nc.scalar.copy
            y_grouped = keep.tile([P, P, PACK], BF16, name="y_grouped%d" % j, align_bytes=64)
            cast(out=y_grouped[:], in_=bank[:].rearrange("p r t -> p t r"))
            return y_grouped

        def round_kept_y(y_grouped, y_kept):
            nc.vector.tensor_copy(
                out=y_grouped.rearrange("p (c i) r -> p c r i", i=4), in_=y_kept.rearrange("p r (c i) -> p c r i", i=4)
            )

        def planes_of_y(y_codes, first_token, y_grouped):
            tokens = y_grouped.shape[1]
            nc.vector.quantize_mx(
                out=y_codes.bitcast(E4M3X4),
                scales=y_plane[:, first_token : first_token + tokens],
                in_=y_grouped.rearrange("p t r -> p (t r)"),
            )

        grouped = None
        for j in range(TILES):
            firsts = [gather_first(j, h) for h in range(2)]
            tag = "codes%d" % (j - 2) if j >= 2 else "pairs%d" % j
            pairs = keep.tile([P, I], BF16, name="pw_pairs%d" % j, tag=tag, align_bytes=64)
            gather_second(j, 0, firsts[0], pairs)
            if j == TILES - 1:
                bank = linear_part(j - 1)
                pair_part(j - 1, grouped, bank)
            gather_second(j, 1, firsts[1], pairs)
            previous = grouped
            grouped = turn(j, pairs)
            if 0 < j < TILES - 1:
                if j == 1:
                    deal_words()
                    deal_scales()
                bank = linear_part(j - 1)
                pair_part(j - 1, previous, bank)
                keep_y(j - 1, bank[0])
                if j == 1:
                    y_grouped0 = round_y(0, bank[0])
        last_bank = linear_part(TILES - 1)
        pair_part(TILES - 1, grouped, last_bank)
        y_grouped1 = shared.tile([P, P, PACK], BF16, name="y_grouped1", offset=B_BASE + 256, align_bytes=64)
        round_kept_y(y_grouped1[:], y_tiles[STORE_GROUPS[0]][:, :, P:])
        y_codes01 = shared.tile([P, 2 * P], I32, name="y_codes01", offset=B_BASE + 256 - 8 * P, align_bytes=64)
        planes_of_y(y_codes01[:, :P], 0, y_grouped0[:])
        y_grouped2 = round_y(2, bank[0])
        keep_y(2, bank[0])
        planes_of_y(y_codes01[:, P:], P, y_grouped1[:])
        nc.sync.dma_start(out=out_words[:, : 2 * P], in_=y_codes01[:])
        y_codes2 = keep.tile([P, P], I32, name="y_codes2", align_bytes=64)
        planes_of_y(y_codes2[:], 2 * P, y_grouped2[:])
        nc.sync.dma_start(out=out_words[:, 2 * P : 3 * P], in_=y_codes2[:])
        last = STORE_GROUPS[2]
        y_last = y_tiles[last]
        nc.vector.tensor_copy(out=y_last[:, 0:2, :], in_=last_bank[0][:])
        nc.scalar.copy(out=y_last[:, 2:4, :], in_=last_bank[1][:])
        nc.sync.dma_start(out=out_rows[:, :, last[0] * P :], in_=y_last[:])
        y_grouped3 = keep.tile([P, P, PACK], BF16, name="y_grouped3", align_bytes=64)
        y_codes3 = keep.tile([P, P], I32, name="y_codes3", align_bytes=64)
        halves = [slice(h * P // 2, (h + 1) * P // 2) for h in range(2)]
        for tokens in halves:
            round_kept_y(y_grouped3[:, tokens, :], y_last[:, :, tokens])
        for tokens in halves:
            planes_of_y(y_codes3[:, tokens], last[0] * P + tokens.start, y_grouped3[:, tokens, :])
        nc.sync.dma_start(out=out_words[:, last[0] * P :], in_=y_codes3[:])

        for q in range(4):
            queue = nc.sync if q % 2 == 0 else nc.scalar
            queue.dma_start(
                out=out_2[0, 4 * q : 4 * q + 4, :].bitcast(I32), in_=y_plane[32 * q : 32 * q + 4, :].bitcast(I32)
            )
